import numpy as np, ml_dtypes
CORES = [1,129,9,137,57,185,105,233,113,241,121,249]
N = 12
VB, TK = 1, 128
def setup_inputs(rng):
    h = rng.standard_normal((128, TK), dtype=np.float32) / 4; w = rng.standard_normal((N, 128, VB * 128), dtype=np.float32)
    a = 2 * np.pi * rng.random((TK)); s = 400 * rng.random((TK)) ** 1.5; h[0] = s * np.cos(a); h[1] = s * np.sin(a); h[2] = 150 * rng.standard_normal((TK)); w[:, 2, :] = 1 + w[:, 2, :] / 50
    a = (2 * np.pi * rng.random() + np.pi / 2 * (rng.permutation(N).reshape(N, 1, 1) + 0.5) / N - 0.5 + (np.arange(VB).reshape(1, VB, 1) + rng.random((N, VB, 128))) / VB).reshape(N, VB * 128); w[:, 0, :] = np.cos(a); w[:, 1, :] = np.sin(a)
    tgt = rng.integers(0, N * VB * 128, size=TK)
    oh = np.zeros((N * VB * 128, TK), np.float32); oh[tgt, np.arange(TK)] = 1.0
    oh = oh.reshape(N, VB, 128, TK).transpose(0, 2, 1, 3).reshape(N, 128, VB * TK)
    return {"h": np.broadcast_to(h, (N, 128, TK)).astype(ml_dtypes.bfloat16), "w": w.astype(ml_dtypes.bfloat16), "oh": oh.astype(ml_dtypes.bfloat16)}
def reference(h, w, oh):
    H, W, OH = h.astype(np.float64), w.astype(np.float64), oh.astype(np.float64)
    Z = np.concatenate([W[r].T @ H[r] for r in range(N)], axis=0)
    O = np.concatenate([OH[r][:, TK * b:TK * b + TK] for r in range(N) for b in range(VB)], axis=0)
    m = Z.max(axis=0)
    P = np.exp(Z - m); P = P / P.sum(axis=0)
    G = P - O
    d = sum(W[r] @ G[VB * 128 * r:VB * 128 * (r + 1)] for r in range(N)).astype(ml_dtypes.bfloat16)
    return {"d": np.broadcast_to(d, (N,) + d.shape)}

@@ -1,0 +1,237 @@
+from concourse.bass import DstId, RemoteDMATransfer
+from concourse.mybir import AluOpType, AxisListType, ActivationFunctionType
+
+NSIM = 256
+PW, CS, CM, CT = 258, 128, 129, 130
+RMAX = 8
+
+SCRATCH = {
+    "h_sb": ("sbuf", [128, 128], "bfloat16"),
+    "w_sb": ("sbuf", [128, 128], "bfloat16"),
+    "oh_sb": ("sbuf", [128, 128], "bfloat16"),
+    "ones": ("sbuf", [128, 128], "bfloat16"),
+    "ident": ("sbuf", [128, 128], "bfloat16"),
+    "wT1": ("sbuf", [128, 136], "bfloat16"),
+    "eT_sb": ("sbuf", [128, 128], "bfloat16"),
+    "e_sb": ("sbuf", [128, 128], "bfloat16"),
+    "pay": ("sbuf", [128, PW], "bfloat16"),
+    "land": ("sbuf", [128, RMAX * PW], "bfloat16"),
+    "fin": ("sbuf", [128, 2 * PW], "bfloat16"),
+    "cw": ("sbuf", [128, RMAX], "float32"),
+    "diag": ("sbuf", [128, RMAX * 128], "bfloat16"),
+    "nm": ("sbuf", [128, 1], "float32"),
+    "cs": ("sbuf", [128, 2], "float32"),
+    "ssum": ("sbuf", [128, 1], "float32"),
+    "rs": ("sbuf", [128, 1], "float32"),
+    "d_sb": ("sbuf", [128, 128], "bfloat16"),
+    "z_ps": ("psum", [128, 512], "float32"),
+    "wT_ps": ("psum", [128, 1024], "bfloat16"),
+    "e_ps": ("psum", [128, 1024], "bfloat16"),
+    "D_ps": ("psum", [128, 512], "float32"),
+    "T_ps": ("psum", [128, 512], "float32"),
+    "f_ps": ("psum", [128, 512], "float32"),
+}
+SEMAPHORES = ["ones", "id", "onec", "ldw", "ldh", "ldoh", "z", "wTp", "wTs", "mu", "eT", "ep", "e", "D", "payD", "Tp", "payT",
+              "sent", "arr1", "arr2", "f1", "f2", "f3", "f4", "f5", "fd", "dsb", "st", "cexp"] + ["dg%d" % i for i in range(RMAX)]
+
+ALU, ACT, AX = AluOpType, ActivationFunctionType, AxisListType
+
+
+def _take(mask, n):
+    out, left = 0, n
+    for i in range(mask.bit_length()):
+        if left and (mask >> i) & 1:
+            out |= 1 << i
+            left -= 1
+    return out
+
+
+def _count(mask):
+    return sum((mask >> i) & 1 for i in range(mask.bit_length()))
+
+
+def _plan(cores, topo):
+    planes = []
+    for c in cores:
+        for p in planes:
+            if topo.same_plane(p[0], c):
+                p.append(c)
+                break
+        else:
+            planes.append([c])
+    mate = {a: b for a in cores for b in cores if topo.mates(a, b)}
+    lone = [c for c in cores if c not in mate]
+    combs = []
+    for pi, p in enumerate(planes):
+        seats = [a for a in p if a in mate]
+        for i, a in enumerate(seats):
+            x = [x for x in range(NSIM)
+                 if topo.host(x) == topo.host(a) and topo.chip(x) == topo.chip(a) and topo.die(x) == topo.die(a)
+                 and x not in cores and topo.may_write(x, mate[a])][0]
+            combs.append((x, pi, [a, mate[a]] + [l for j, l in enumerate(lone) if j % len(seats) == i]))
+    return planes, combs
+
+
+def _hop2(x, dests, topo):
+    full = topo.mask(x, dests[0])
+    low = full
+    for d in dests[1:]:
+        low &= topo.mask(x, d)
+    return [(_take(full & ~low, 4), dests[:1]), (low, dests[1:])]
+
+
+def _dst(d, src, topo):
+    rid, pid = topo.addr(d, src)
+    return DstId(rid=rid, pnc=pid)
+
+
+def _identity(g, T):
+    g.vector.memset(T.ones[:], 1.0).then_inc(T.sem.ones, 1)
+    g.wait_ge(T.sem.ones, 1)
+    g.affine_select(T.ident[:], T.ones[:], [[-1, 128]], ALU.is_equal, 0.0, 0, 1).then_inc(T.sem.id, 1)
+
+
+def _combiner(g, core, T, topo, srcs, pi, dests):
+    S, R = T.sem, len(srcs)
+    v, s, t = g.vector, g.scalar, g.tensor
+    need = 0
+    for c in srcs:
+        need += _count(_rank_mask(c, topo, T))
+    _identity(g, T)
+    mus = T.land[:, CM:CM + PW * (R - 1) + 1:PW]
+    v.wait_ge(S.arr1, need)
+    v.tensor_reduce(T.pay[:, CM:CM + 1], mus, AX.X, ALU.min).then_inc(S.mu, 1)
+    s.wait_ge(S.arr1, need)
+    s.wait_ge(S.mu, 1)
+    s.activation(T.cw[:, 0:R], mus, ACT.Exp, bias=T.pay[:, CM:CM + 1], scale=-1.0).then_inc(S.cexp, 1)
+    t.wait_ge(S.arr1, need)
+    t.wait_ge(S.id, 1)
+    for r in range(R):
+        t.matmul(T.T_ps[:, 0:128], T.ident[:], T.land[:, r * PW + CT:r * PW + PW], r == 0, r == R - 1).then_inc(S.Tp, 1)
+    v.wait_ge(S.id, 1)
+    v.wait_ge(S.cexp, 1)
+    s.wait_ge(S.id, 1)
+    s.wait_ge(S.cexp, 1)
+    for r in range(R):
+        o = T.diag[:, r * 128:(r + 1) * 128]
+        if r % 2 == 0:
+            v.tensor_scalar(o, T.ident[:], T.cw[:, r:r + 1], None, ALU.mult).then_inc(S["dg%d" % r], 1)
+        else:
+            s.activation(o, T.ident[:], ACT.Copy, scale=T.cw[:, r:r + 1]).then_inc(S["dg%d" % r], 1)
+    for r in range(R):
+        t.wait_ge(S["dg%d" % r], 1)
+        t.matmul(T.D_ps[:, 0:CM], T.diag[:, r * 128:(r + 1) * 128], T.land[:, r * PW:r * PW + CM], r == 0, r == R - 1).then_inc(S.D, 1)
+    s.wait_ge(S.Tp, R)
+    s.activation(T.pay[:, CT:PW], T.T_ps[:, 0:128], ACT.Copy).then_inc(S.payT, 1)
+    v.wait_ge(S.D, R)
+    v.tensor_copy(T.pay[:, 0:CM], T.D_ps[:, 0:CM]).then_inc(S.payD, 1)
+    g.wait_ge(S.mu, 1)
+    g.wait_ge(S.payT, 1)
+    g.wait_ge(S.payD, 1)
+    trs, sent = [], 0
+    for m, ds in _hop2(core, dests, topo):
+        trs.append(RemoteDMATransfer(dst_ids=[_dst(d, core, topo) for d in ds], dma_engine_mask=m, remote_sem=S.arr2,
+                                     srcs=[T.pay[:]], dsts=[T.fin[:, pi * PW:(pi + 1) * PW] for d in ds], alu_op=0))
+        sent += _count(m)
+    g.remote_dma_fused(trs, local_sem=S.sent)
+    g.wait_ge(S.sent, sent)
+
+
+def _rank_mask(c, topo, T):
+    planes, combs = _plan(T.cores, topo)
+    m = None
+    for x, pi, ds in combs:
+        if c in planes[pi]:
+            m = topo.mask(c, x) if m is None else m & topo.mask(c, x)
+    return m
+
+
+def rank_program(g, core, T, topo):
+    planes, combs = _plan(T.cores, topo)
+    for x, pi, ds in combs:
+        if x == core:
+            _combiner(g, core, T, topo, planes[pi], pi, ds)
+            return
+    if T.rank_of(core) is None:
+        return
+    S = T.sem
+    v, s, t = g.vector, g.scalar, g.tensor
+    mine = [pi for pi, p in enumerate(planes) if core in p][0]
+    slot = planes[mine].index(core)
+
+    g.sync.dma_start(T.w_sb[:], T.w[:]).then_inc(S.ldw, 16)
+    s.dma_start(T.h_sb[:], T.h[:]).then_inc(S.ldh, 16)
+    g.sync.dma_start(T.oh_sb[:], T.oh[:]).then_inc(S.ldoh, 16)
+    _identity(g, T)
+    v.memset(T.wT1[:, 128:129], 1.0).then_inc(S.onec, 1)
+
+    t.wait_ge(S.ldw, 16)
+    t.wait_ge(S.ldh, 16)
+    t.matmul(T.z_ps[:, 0:128], T.h_sb[:], T.w_sb[:], True, True).then_inc(S.z, 1)
+    t.wait_ge(S.id, 1)
+    t.transpose(T.wT_ps[:, 0:128], T.w_sb[:], T.ident[:]).then_inc(S.wTp, 1)
+    v.wait_ge(S.z, 1)
+    v.tensor_reduce(T.pay[:, CM:CM + 1], T.z_ps[:, 0:128], AX.X, ALU.max, negate=True).then_inc(S.mu, 1)
+    s.wait_ge(S.mu, 1)
+    s.activation(T.eT_sb[:], T.z_ps[:, 0:128], ACT.Exp, bias=T.pay[:, CM:CM + 1]).then_inc(S.eT, 1)
+    v.wait_ge(S.wTp, 1)
+    v.tensor_copy(T.wT1[:, 0:128], T.wT_ps[:, 0:128]).then_inc(S.wTs, 1)
+    t.wait_ge(S.wTs, 1)
+    t.wait_ge(S.ldoh, 16)
+    t.matmul(T.T_ps[:, 0:128], T.oh_sb[:], T.wT1[:, 0:128], True, True).then_inc(S.Tp, 1)
+    v.wait_ge(S.Tp, 1)
+    v.tensor_scalar(T.pay[:, CT:PW], T.T_ps[:, 0:128], -1.0, None, ALU.mult).then_inc(S.payT, 1)
+    t.wait_ge(S.eT, 1)
+    t.transpose(T.e_ps[:, 0:128], T.eT_sb[:], T.ident[:]).then_inc(S.ep, 1)
+    v.wait_ge(S.ep, 1)
+    v.tensor_copy(T.e_sb[:], T.e_ps[:, 0:128]).then_inc(S.e, 1)
+    t.wait_ge(S.e, 1)
+    t.wait_ge(S.onec, 1)
+    t.matmul(T.D_ps[:, 0:CM], T.e_sb[:], T.wT1[:, 0:CM], True, True).then_inc(S.D, 1)
+    v.wait_ge(S.D, 1)
+    v.tensor_copy(T.pay[:, 0:CM], T.D_ps[:, 0:CM]).then_inc(S.payD, 1)
+
+    g.wait_ge(S.mu, 1)
+    g.wait_ge(S.payT, 1)
+    g.wait_ge(S.payD, 1)
+    to = [x for x, pi, ds in combs if pi == mine]
+    m = _rank_mask(core, topo, T)
+    g.remote_dma_fused([RemoteDMATransfer(dst_ids=[_dst(x, core, topo) for x in to], dma_engine_mask=m, remote_sem=S.arr1,
+                                          srcs=[T.pay[:]], dsts=[T.land[:, slot * PW:(slot + 1) * PW] for x in to], alu_op=0)],
+                       local_sem=S.sent)
+
+    need = 0
+    for x, pi, ds in combs:
+        for mk, dd in _hop2(x, ds, topo):
+            if core in dd:
+                need += _count(mk)
+    mus = T.fin[:, CM:CM + PW + 1:PW]
+    ss = T.fin[:, CS:CS + PW + 1:PW]
+    t.wait_ge(S.arr2, need)
+    t.matmul(T.f_ps[:, 0:128], T.fin[:, CT:PW], T.ident[:], True, False)
+    t.matmul(T.f_ps[:, 0:128], T.fin[:, PW + CT:2 * PW], T.ident[:], False, False)
+    v.wait_ge(S.arr2, need)
+    v.tensor_reduce(T.nm[:], mus, AX.X, ALU.min).then_inc(S.f1, 1)
+    s.wait_ge(S.arr2, need)
+    s.wait_ge(S.f1, 1)
+    s.activation(T.cw[:, 0:2], mus, ACT.Exp, bias=T.nm[:], scale=-1.0).then_inc(S.f2, 1)
+    v.wait_ge(S.f2, 1)
+    v.tensor_tensor(T.cs[:], T.cw[:, 0:2], ss, ALU.mult).then_inc(S.f3, 1)
+    v.wait_ge(S.f3, 1)
+    v.tensor_reduce(T.ssum[:], T.cs[:], AX.X, ALU.add).then_inc(S.f4, 1)
+    v.wait_ge(S.f4, 1)
+    v.reciprocal(T.rs[:], T.ssum[:]).then_inc(S.f5, 1)
+    v.wait_ge(S.f5, 1)
+    v.wait_ge(S.id, 1)
+    for p in range(2):
+        v.tensor_scalar(T.diag[:, p * 128:(p + 1) * 128], T.ident[:], T.cw[:, p:p + 1], T.rs[:], ALU.mult, ALU.mult).then_inc(S["dg%d" % p], 1)
+    for p in range(2):
+        t.wait_ge(S["dg%d" % p], 1)
+        i = t.matmul(T.f_ps[:, 0:128], T.fin[:, p * PW:p * PW + 128], T.diag[:, p * 128:(p + 1) * 128], False, p == 1)
+    i.then_inc(S.fd, 1)
+    v.wait_ge(S.fd, 1)
+    v.tensor_copy(T.d_sb[:], T.f_ps[:, 0:128]).then_inc(S.dsb, 1)
+    g.sync.wait_ge(S.dsb, 1)
+    g.sync.dma_start(T.d[:], T.d_sb[:]).then_inc(S.st, 16)
+    g.sync.wait_ge(S.st, 16)
+    g.wait_ge(S.sent, _count(m))

@@ -2,7 +2,7 @@ from concourse.bass import DstId, RemoteDMATransfer
 from concourse.mybir import AluOpType, AxisListType, ActivationFunctionType
 
 NSIM = 256
-PW, CS, CM, CT = 258, 128, 129, 130
+PW, CS, CM = 130, 128, 129
 RMAX = 8
 
 SCRATCH = {
@@ -15,8 +15,11 @@ SCRATCH = {
     "eT_sb": ("sbuf", [128, 128], "bfloat16"),
     "e_sb": ("sbuf", [128, 128], "bfloat16"),
     "pay": ("sbuf", [128, PW], "bfloat16"),
+    "payT": ("sbuf", [128, 128], "bfloat16"),
     "land": ("sbuf", [128, RMAX * PW], "bfloat16"),
+    "landT": ("sbuf", [128, RMAX * 128], "bfloat16"),
     "fin": ("sbuf", [128, 2 * PW], "bfloat16"),
+    "finT": ("sbuf", [128, 2 * 128], "bfloat16"),
     "cw": ("sbuf", [128, RMAX], "float32"),
     "diag": ("sbuf", [128, RMAX * 128], "bfloat16"),
     "nm": ("sbuf", [128, 1], "float32"),
@@ -32,7 +35,8 @@ SCRATCH = {
     "f_ps": ("psum", [128, 512], "float32"),
 }
 SEMAPHORES = ["ones", "id", "onec", "ldw", "ldh", "ldoh", "z", "wTp", "wTs", "mu", "eT", "ep", "e", "D", "payD", "Tp", "payT",
-              "sent", "arr1", "arr2", "f1", "f2", "f3", "f4", "f5", "fd", "dsb", "st", "cexp"] + ["dg%d" % i for i in range(RMAX)]
+              "sent", "arr1", "arr2", "arrT1", "arrT2", "f1", "f2", "f3", "f4", "f5", "fd", "dsb", "st", "cexp"] \
+             + ["dg%d" % i for i in range(RMAX)]
 
 ALU, ACT, AX = AluOpType, ActivationFunctionType, AxisListType
 
@@ -91,6 +95,15 @@ def _identity(g, T):
     g.affine_select(T.ident[:], T.ones[:], [[-1, 128]], ALU.is_equal, 0.0, 0, 1).then_inc(T.sem.id, 1)
 
 
+def _rank_mask(c, topo, T):
+    planes, combs = _plan(T.cores, topo)
+    m = None
+    for x, pi, ds in combs:
+        if c in planes[pi]:
+            m = topo.mask(c, x) if m is None else m & topo.mask(c, x)
+    return m
+
+
 def _combiner(g, core, T, topo, srcs, pi, dests):
     S, R = T.sem, len(srcs)
     v, s, t = g.vector, g.scalar, g.tensor
@@ -99,15 +112,25 @@ def _combiner(g, core, T, topo, srcs, pi, dests):
         need += _count(_rank_mask(c, topo, T))
     _identity(g, T)
     mus = T.land[:, CM:CM + PW * (R - 1) + 1:PW]
+
+    def send(src, dst, sem):
+        g.remote_dma_fused([RemoteDMATransfer(dst_ids=[_dst(d, core, topo) for d in ds], dma_engine_mask=m, remote_sem=sem,
+                                              srcs=[src], dsts=[dst for d in ds], alu_op=0)
+                            for m, ds in _hop2(core, dests, topo)], local_sem=S.sent)
+
+    t.wait_ge(S.arrT1, need)
+    t.wait_ge(S.id, 1)
+    for r in range(R):
+        t.matmul(T.T_ps[:, 0:128], T.ident[:], T.landT[:, r * 128:(r + 1) * 128], r == 0, r == R - 1).then_inc(S.Tp, 1)
+    v.wait_ge(S.Tp, R)
+    v.tensor_copy(T.payT[:], T.T_ps[:, 0:128]).then_inc(S.payT, 1)
+    g.wait_ge(S.payT, 1)
+    send(T.payT[:], T.finT[:, pi * 128:(pi + 1) * 128], S.arrT2)
     v.wait_ge(S.arr1, need)
     v.tensor_reduce(T.pay[:, CM:CM + 1], mus, AX.X, ALU.min).then_inc(S.mu, 1)
     s.wait_ge(S.arr1, need)
     s.wait_ge(S.mu, 1)
     s.activation(T.cw[:, 0:R], mus, ACT.Exp, bias=T.pay[:, CM:CM + 1], scale=-1.0).then_inc(S.cexp, 1)
-    t.wait_ge(S.arr1, need)
-    t.wait_ge(S.id, 1)
-    for r in range(R):
-        t.matmul(T.T_ps[:, 0:128], T.ident[:], T.land[:, r * PW + CT:r * PW + PW], r == 0, r == R - 1).then_inc(S.Tp, 1)
     v.wait_ge(S.id, 1)
     v.wait_ge(S.cexp, 1)
     s.wait_ge(S.id, 1)
@@ -118,32 +141,16 @@ def _combiner(g, core, T, topo, srcs, pi, dests):
             v.tensor_scalar(o, T.ident[:], T.cw[:, r:r + 1], None, ALU.mult).then_inc(S["dg%d" % r], 1)
         else:
             s.activation(o, T.ident[:], ACT.Copy, scale=T.cw[:, r:r + 1]).then_inc(S["dg%d" % r], 1)
+    t.wait_ge(S.arr1, need)
     for r in range(R):
         t.wait_ge(S["dg%d" % r], 1)
         t.matmul(T.D_ps[:, 0:CM], T.diag[:, r * 128:(r + 1) * 128], T.land[:, r * PW:r * PW + CM], r == 0, r == R - 1).then_inc(S.D, 1)
-    s.wait_ge(S.Tp, R)
-    s.activation(T.pay[:, CT:PW], T.T_ps[:, 0:128], ACT.Copy).then_inc(S.payT, 1)
     v.wait_ge(S.D, R)
     v.tensor_copy(T.pay[:, 0:CM], T.D_ps[:, 0:CM]).then_inc(S.payD, 1)
     g.wait_ge(S.mu, 1)
-    g.wait_ge(S.payT, 1)
     g.wait_ge(S.payD, 1)
-    trs, sent = [], 0
-    for m, ds in _hop2(core, dests, topo):
-        trs.append(RemoteDMATransfer(dst_ids=[_dst(d, core, topo) for d in ds], dma_engine_mask=m, remote_sem=S.arr2,
-                                     srcs=[T.pay[:]], dsts=[T.fin[:, pi * PW:(pi + 1) * PW] for d in ds], alu_op=0))
-        sent += _count(m)
-    g.remote_dma_fused(trs, local_sem=S.sent)
-    g.wait_ge(S.sent, sent)
-
-
-def _rank_mask(c, topo, T):
-    planes, combs = _plan(T.cores, topo)
-    m = None
-    for x, pi, ds in combs:
-        if c in planes[pi]:
-            m = topo.mask(c, x) if m is None else m & topo.mask(c, x)
-    return m
+    send(T.pay[:], T.fin[:, pi * PW:(pi + 1) * PW], S.arr2)
+    g.wait_ge(S.sent, 2 * sum(_count(m) for m, ds in _hop2(core, dests, topo)))
 
 
 def rank_program(g, core, T, topo):
@@ -180,7 +187,7 @@ def rank_program(g, core, T, topo):
     t.wait_ge(S.ldoh, 16)
     t.matmul(T.T_ps[:, 0:128], T.oh_sb[:], T.wT1[:, 0:128], True, True).then_inc(S.Tp, 1)
     v.wait_ge(S.Tp, 1)
-    v.tensor_scalar(T.pay[:, CT:PW], T.T_ps[:, 0:128], -1.0, None, ALU.mult).then_inc(S.payT, 1)
+    v.tensor_scalar(T.payT[:], T.T_ps[:, 0:128], -1.0, None, ALU.mult).then_inc(S.payT, 1)
     t.wait_ge(S.eT, 1)
     t.transpose(T.e_ps[:, 0:128], T.eT_sb[:], T.ident[:]).then_inc(S.ep, 1)
     v.wait_ge(S.ep, 1)
@@ -191,14 +198,18 @@ def rank_program(g, core, T, topo):
     v.wait_ge(S.D, 1)
     v.tensor_copy(T.pay[:, 0:CM], T.D_ps[:, 0:CM]).then_inc(S.payD, 1)
 
-    g.wait_ge(S.mu, 1)
-    g.wait_ge(S.payT, 1)
-    g.wait_ge(S.payD, 1)
     to = [x for x, pi, ds in combs if pi == mine]
     m = _rank_mask(core, topo, T)
-    g.remote_dma_fused([RemoteDMATransfer(dst_ids=[_dst(x, core, topo) for x in to], dma_engine_mask=m, remote_sem=S.arr1,
-                                          srcs=[T.pay[:]], dsts=[T.land[:, slot * PW:(slot + 1) * PW] for x in to], alu_op=0)],
-                       local_sem=S.sent)
+
+    def send(src, dst, sem):
+        g.remote_dma_fused([RemoteDMATransfer(dst_ids=[_dst(x, core, topo) for x in to], dma_engine_mask=m, remote_sem=sem,
+                                              srcs=[src], dsts=[dst for x in to], alu_op=0)], local_sem=S.sent)
+
+    g.wait_ge(S.payT, 1)
+    send(T.payT[:], T.landT[:, slot * 128:(slot + 1) * 128], S.arrT1)
+    g.wait_ge(S.mu, 1)
+    g.wait_ge(S.payD, 1)
+    send(T.pay[:], T.land[:, slot * PW:(slot + 1) * PW], S.arr1)
 
     need = 0
     for x, pi, ds in combs:
@@ -207,9 +218,10 @@ def rank_program(g, core, T, topo):
                 need += _count(mk)
     mus = T.fin[:, CM:CM + PW + 1:PW]
     ss = T.fin[:, CS:CS + PW + 1:PW]
+    t.wait_ge(S.arrT2, need)
+    t.matmul(T.f_ps[:, 0:128], T.finT[:, 0:128], T.ident[:], True, False)
+    t.matmul(T.f_ps[:, 0:128], T.finT[:, 128:256], T.ident[:], False, False)
     t.wait_ge(S.arr2, need)
-    t.matmul(T.f_ps[:, 0:128], T.fin[:, CT:PW], T.ident[:], True, False)
-    t.matmul(T.f_ps[:, 0:128], T.fin[:, PW + CT:2 * PW], T.ident[:], False, False)
     v.wait_ge(S.arr2, need)
     v.tensor_reduce(T.nm[:], mus, AX.X, ALU.min).then_inc(S.f1, 1)
     s.wait_ge(S.arr2, need)
@@ -234,4 +246,4 @@ def rank_program(g, core, T, topo):
     g.sync.wait_ge(S.dsb, 1)
     g.sync.dma_start(T.d[:], T.d_sb[:]).then_inc(S.st, 16)
     g.sync.wait_ge(S.st, 16)
-    g.wait_ge(S.sent, _count(m))
+    g.wait_ge(S.sent, 2 * _count(m))

@@ -2,7 +2,7 @@ from concourse.bass import DstId, RemoteDMATransfer
 from concourse.mybir import AluOpType, AxisListType, ActivationFunctionType
 
 NSIM = 256
-PW, CS, CM = 130, 128, 129
+PW = 129
 RMAX = 8
 
 SCRATCH = {
@@ -15,13 +15,14 @@ SCRATCH = {
     "eT_sb": ("sbuf", [128, 128], "bfloat16"),
     "e_sb": ("sbuf", [128, 128], "bfloat16"),
     "pay": ("sbuf", [128, PW], "bfloat16"),
-    "payT": ("sbuf", [128, 128], "bfloat16"),
+    "payT": ("sbuf", [128, PW], "bfloat16"),
     "land": ("sbuf", [128, RMAX * PW], "bfloat16"),
-    "landT": ("sbuf", [128, RMAX * 128], "bfloat16"),
+    "landT": ("sbuf", [128, RMAX * PW], "bfloat16"),
     "fin": ("sbuf", [128, 2 * PW], "bfloat16"),
-    "finT": ("sbuf", [128, 2 * 128], "bfloat16"),
+    "finT": ("sbuf", [128, 2 * PW], "bfloat16"),
     "cw": ("sbuf", [128, RMAX], "float32"),
     "diag": ("sbuf", [128, RMAX * 128], "bfloat16"),
+    "dq": ("sbuf", [128, 2 * 128], "bfloat16"),
     "nm": ("sbuf", [128, 1], "float32"),
     "cs": ("sbuf", [128, 2], "float32"),
     "ssum": ("sbuf", [128, 1], "float32"),
@@ -35,8 +36,8 @@ SCRATCH = {
     "f_ps": ("psum", [128, 512], "float32"),
 }
 SEMAPHORES = ["ones", "id", "onec", "ldw", "ldh", "ldoh", "z", "wTp", "wTs", "mu", "eT", "ep", "e", "D", "payD", "Tp", "payT",
-              "sent", "arr1", "arr2", "arrT1", "arrT2", "f1", "f2", "f3", "f4", "f5", "fd", "dsb", "st", "cexp"] \
-             + ["dg%d" % i for i in range(RMAX)]
+              "sent", "arr2", "arrT2", "q0", "q1", "f1", "f2", "f3", "f4", "f5", "fd", "dsb", "st", "cexp"] \
+             + [n % i for i in range(RMAX) for n in ("dg%d", "aT%d", "aD%d")]
 
 ALU, ACT, AX = AluOpType, ActivationFunctionType, AxisListType
 
@@ -107,30 +108,30 @@ def _rank_mask(c, topo, T):
 def _combiner(g, core, T, topo, srcs, pi, dests):
     S, R = T.sem, len(srcs)
     v, s, t = g.vector, g.scalar, g.tensor
-    need = 0
-    for c in srcs:
-        need += _count(_rank_mask(c, topo, T))
+    need = [_count(_rank_mask(c, topo, T)) for c in srcs]
     _identity(g, T)
-    mus = T.land[:, CM:CM + PW * (R - 1) + 1:PW]
+    mus = T.landT[:, 128:128 + PW * (R - 1) + 1:PW]
 
     def send(src, dst, sem):
         g.remote_dma_fused([RemoteDMATransfer(dst_ids=[_dst(d, core, topo) for d in ds], dma_engine_mask=m, remote_sem=sem,
                                               srcs=[src], dsts=[dst for d in ds], alu_op=0)
                             for m, ds in _hop2(core, dests, topo)], local_sem=S.sent)
 
-    t.wait_ge(S.arrT1, need)
     t.wait_ge(S.id, 1)
     for r in range(R):
-        t.matmul(T.T_ps[:, 0:128], T.ident[:], T.landT[:, r * 128:(r + 1) * 128], r == 0, r == R - 1).then_inc(S.Tp, 1)
+        t.wait_ge(S["aT%d" % r], need[r])
+        t.matmul(T.T_ps[:, 0:128], T.ident[:], T.landT[:, r * PW:r * PW + 128], r == 0, r == R - 1).then_inc(S.Tp, 1)
+    for r in range(R):
+        v.wait_ge(S["aT%d" % r], need[r])
+        s.wait_ge(S["aT%d" % r], need[r])
+    v.tensor_reduce(T.payT[:, 128:129], mus, AX.X, ALU.min).then_inc(S.mu, 1)
     v.wait_ge(S.Tp, R)
-    v.tensor_copy(T.payT[:], T.T_ps[:, 0:128]).then_inc(S.payT, 1)
+    v.tensor_copy(T.payT[:, 0:128], T.T_ps[:, 0:128]).then_inc(S.payT, 1)
+    g.wait_ge(S.mu, 1)
     g.wait_ge(S.payT, 1)
-    send(T.payT[:], T.finT[:, pi * 128:(pi + 1) * 128], S.arrT2)
-    v.wait_ge(S.arr1, need)
-    v.tensor_reduce(T.pay[:, CM:CM + 1], mus, AX.X, ALU.min).then_inc(S.mu, 1)
-    s.wait_ge(S.arr1, need)
+    send(T.payT[:], T.finT[:, pi * PW:(pi + 1) * PW], S.arrT2)
     s.wait_ge(S.mu, 1)
-    s.activation(T.cw[:, 0:R], mus, ACT.Exp, bias=T.pay[:, CM:CM + 1], scale=-1.0).then_inc(S.cexp, 1)
+    s.activation(T.cw[:, 0:R], mus, ACT.Exp, bias=T.payT[:, 128:129], scale=-1.0).then_inc(S.cexp, 1)
     v.wait_ge(S.id, 1)
     v.wait_ge(S.cexp, 1)
     s.wait_ge(S.id, 1)
@@ -141,13 +142,12 @@ def _combiner(g, core, T, topo, srcs, pi, dests):
             v.tensor_scalar(o, T.ident[:], T.cw[:, r:r + 1], None, ALU.mult).then_inc(S["dg%d" % r], 1)
         else:
             s.activation(o, T.ident[:], ACT.Copy, scale=T.cw[:, r:r + 1]).then_inc(S["dg%d" % r], 1)
-    t.wait_ge(S.arr1, need)
     for r in range(R):
         t.wait_ge(S["dg%d" % r], 1)
-        t.matmul(T.D_ps[:, 0:CM], T.diag[:, r * 128:(r + 1) * 128], T.land[:, r * PW:r * PW + CM], r == 0, r == R - 1).then_inc(S.D, 1)
+        t.wait_ge(S["aD%d" % r], need[r])
+        t.matmul(T.D_ps[:, 0:PW], T.diag[:, r * 128:(r + 1) * 128], T.land[:, r * PW:(r + 1) * PW], r == 0, r == R - 1).then_inc(S.D, 1)
     v.wait_ge(S.D, R)
-    v.tensor_copy(T.pay[:, 0:CM], T.D_ps[:, 0:CM]).then_inc(S.payD, 1)
-    g.wait_ge(S.mu, 1)
+    v.tensor_copy(T.pay[:], T.D_ps[:, 0:PW]).then_inc(S.payD, 1)
     g.wait_ge(S.payD, 1)
     send(T.pay[:], T.fin[:, pi * PW:(pi + 1) * PW], S.arr2)
     g.wait_ge(S.sent, 2 * sum(_count(m) for m, ds in _hop2(core, dests, topo)))
@@ -178,25 +178,25 @@ def rank_program(g, core, T, topo):
     t.wait_ge(S.id, 1)
     t.transpose(T.wT_ps[:, 0:128], T.w_sb[:], T.ident[:]).then_inc(S.wTp, 1)
     v.wait_ge(S.z, 1)
-    v.tensor_reduce(T.pay[:, CM:CM + 1], T.z_ps[:, 0:128], AX.X, ALU.max, negate=True).then_inc(S.mu, 1)
+    v.tensor_reduce(T.payT[:, 128:129], T.z_ps[:, 0:128], AX.X, ALU.max, negate=True).then_inc(S.mu, 1)
     s.wait_ge(S.mu, 1)
-    s.activation(T.eT_sb[:], T.z_ps[:, 0:128], ACT.Exp, bias=T.pay[:, CM:CM + 1]).then_inc(S.eT, 1)
+    s.activation(T.eT_sb[:], T.z_ps[:, 0:128], ACT.Exp, bias=T.payT[:, 128:129]).then_inc(S.eT, 1)
     v.wait_ge(S.wTp, 1)
     v.tensor_copy(T.wT1[:, 0:128], T.wT_ps[:, 0:128]).then_inc(S.wTs, 1)
     t.wait_ge(S.wTs, 1)
     t.wait_ge(S.ldoh, 16)
     t.matmul(T.T_ps[:, 0:128], T.oh_sb[:], T.wT1[:, 0:128], True, True).then_inc(S.Tp, 1)
     v.wait_ge(S.Tp, 1)
-    v.tensor_scalar(T.payT[:], T.T_ps[:, 0:128], -1.0, None, ALU.mult).then_inc(S.payT, 1)
+    v.tensor_scalar(T.payT[:, 0:128], T.T_ps[:, 0:128], -1.0, None, ALU.mult).then_inc(S.payT, 1)
     t.wait_ge(S.eT, 1)
     t.transpose(T.e_ps[:, 0:128], T.eT_sb[:], T.ident[:]).then_inc(S.ep, 1)
     v.wait_ge(S.ep, 1)
     v.tensor_copy(T.e_sb[:], T.e_ps[:, 0:128]).then_inc(S.e, 1)
     t.wait_ge(S.e, 1)
     t.wait_ge(S.onec, 1)
-    t.matmul(T.D_ps[:, 0:CM], T.e_sb[:], T.wT1[:, 0:CM], True, True).then_inc(S.D, 1)
+    t.matmul(T.D_ps[:, 0:PW], T.e_sb[:], T.wT1[:, 0:PW], True, True).then_inc(S.D, 1)
     v.wait_ge(S.D, 1)
-    v.tensor_copy(T.pay[:, 0:CM], T.D_ps[:, 0:CM]).then_inc(S.payD, 1)
+    v.tensor_copy(T.pay[:], T.D_ps[:, 0:PW]).then_inc(S.payD, 1)
 
     to = [x for x, pi, ds in combs if pi == mine]
     m = _rank_mask(core, topo, T)
@@ -205,41 +205,47 @@ def rank_program(g, core, T, topo):
         g.remote_dma_fused([RemoteDMATransfer(dst_ids=[_dst(x, core, topo) for x in to], dma_engine_mask=m, remote_sem=sem,
                                               srcs=[src], dsts=[dst for x in to], alu_op=0)], local_sem=S.sent)
 
-    g.wait_ge(S.payT, 1)
-    send(T.payT[:], T.landT[:, slot * 128:(slot + 1) * 128], S.arrT1)
     g.wait_ge(S.mu, 1)
+    g.wait_ge(S.payT, 1)
+    send(T.payT[:], T.landT[:, slot * PW:(slot + 1) * PW], S["aT%d" % slot])
     g.wait_ge(S.payD, 1)
-    send(T.pay[:], T.land[:, slot * PW:(slot + 1) * PW], S.arr1)
+    send(T.pay[:], T.land[:, slot * PW:(slot + 1) * PW], S["aD%d" % slot])
 
     need = 0
     for x, pi, ds in combs:
         for mk, dd in _hop2(x, ds, topo):
             if core in dd:
                 need += _count(mk)
-    mus = T.fin[:, CM:CM + PW + 1:PW]
-    ss = T.fin[:, CS:CS + PW + 1:PW]
+    mus = T.finT[:, 128:128 + PW + 1:PW]
+    ss = T.fin[:, 128:128 + PW + 1:PW]
     t.wait_ge(S.arrT2, need)
     t.matmul(T.f_ps[:, 0:128], T.finT[:, 0:128], T.ident[:], True, False)
-    t.matmul(T.f_ps[:, 0:128], T.finT[:, 128:256], T.ident[:], False, False)
-    t.wait_ge(S.arr2, need)
-    v.wait_ge(S.arr2, need)
+    t.matmul(T.f_ps[:, 0:128], T.finT[:, PW:PW + 128], T.ident[:], False, False)
+    v.wait_ge(S.arrT2, need)
     v.tensor_reduce(T.nm[:], mus, AX.X, ALU.min).then_inc(S.f1, 1)
-    s.wait_ge(S.arr2, need)
+    s.wait_ge(S.arrT2, need)
     s.wait_ge(S.f1, 1)
     s.activation(T.cw[:, 0:2], mus, ACT.Exp, bias=T.nm[:], scale=-1.0).then_inc(S.f2, 1)
     v.wait_ge(S.f2, 1)
+    v.wait_ge(S.id, 1)
+    for p in range(2):
+        v.tensor_scalar(T.diag[:, p * 128:(p + 1) * 128], T.ident[:], T.cw[:, p:p + 1], None, ALU.mult).then_inc(S["dg%d" % p], 1)
+    v.wait_ge(S.arr2, need)
     v.tensor_tensor(T.cs[:], T.cw[:, 0:2], ss, ALU.mult).then_inc(S.f3, 1)
     v.wait_ge(S.f3, 1)
     v.tensor_reduce(T.ssum[:], T.cs[:], AX.X, ALU.add).then_inc(S.f4, 1)
     v.wait_ge(S.f4, 1)
     v.reciprocal(T.rs[:], T.ssum[:]).then_inc(S.f5, 1)
     v.wait_ge(S.f5, 1)
-    v.wait_ge(S.id, 1)
+    v.wait_ge(S.dg0, 1)
+    v.tensor_scalar(T.dq[:, 0:128], T.diag[:, 0:128], T.rs[:], None, ALU.mult).then_inc(S.q0, 1)
+    s.wait_ge(S.f5, 1)
+    s.wait_ge(S.dg1, 1)
+    s.activation(T.dq[:, 128:256], T.diag[:, 128:256], ACT.Copy, scale=T.rs[:]).then_inc(S.q1, 1)
+    t.wait_ge(S.arr2, need)
     for p in range(2):
-        v.tensor_scalar(T.diag[:, p * 128:(p + 1) * 128], T.ident[:], T.cw[:, p:p + 1], T.rs[:], ALU.mult, ALU.mult).then_inc(S["dg%d" % p], 1)
-    for p in range(2):
-        t.wait_ge(S["dg%d" % p], 1)
-        i = t.matmul(T.f_ps[:, 0:128], T.fin[:, p * PW:p * PW + 128], T.diag[:, p * 128:(p + 1) * 128], False, p == 1)
+        t.wait_ge(S["q%d" % p], 1)
+        i = t.matmul(T.f_ps[:, 0:128], T.fin[:, p * PW:p * PW + 128], T.dq[:, p * 128:(p + 1) * 128], False, p == 1)
     i.then_inc(S.fd, 1)
     v.wait_ge(S.fd, 1)
     v.tensor_copy(T.d_sb[:], T.f_ps[:, 0:128]).then_inc(S.dsb, 1)

@@ -3,7 +3,7 @@ from concourse.mybir import AluOpType, AxisListType, ActivationFunctionType
 
 NSIM = 256
 PW = 129
-RMAX = 8
+RMAX = 4
 
 SCRATCH = {
     "h_sb": ("sbuf", [128, 128], "bfloat16"),
@@ -18,13 +18,13 @@ SCRATCH = {
     "payT": ("sbuf", [128, PW], "bfloat16"),
     "land": ("sbuf", [128, RMAX * PW], "bfloat16"),
     "landT": ("sbuf", [128, RMAX * PW], "bfloat16"),
-    "fin": ("sbuf", [128, 2 * PW], "bfloat16"),
-    "finT": ("sbuf", [128, 2 * PW], "bfloat16"),
+    "fin": ("sbuf", [128, RMAX * PW], "bfloat16"),
+    "finT": ("sbuf", [128, RMAX * PW], "bfloat16"),
     "cw": ("sbuf", [128, RMAX], "float32"),
     "diag": ("sbuf", [128, RMAX * 128], "bfloat16"),
-    "dq": ("sbuf", [128, 2 * 128], "bfloat16"),
+    "dq": ("sbuf", [128, RMAX * 128], "bfloat16"),
     "nm": ("sbuf", [128, 1], "float32"),
-    "cs": ("sbuf", [128, 2], "float32"),
+    "cs": ("sbuf", [128, RMAX], "float32"),
     "ssum": ("sbuf", [128, 1], "float32"),
     "rs": ("sbuf", [128, 1], "float32"),
     "d_sb": ("sbuf", [128, 128], "bfloat16"),
@@ -36,8 +36,8 @@ SCRATCH = {
     "f_ps": ("psum", [128, 512], "float32"),
 }
 SEMAPHORES = ["ones", "id", "onec", "ldw", "ldh", "ldoh", "z", "wTp", "wTs", "mu", "eT", "ep", "e", "D", "payD", "Tp", "payT",
-              "sent", "arr2", "arrT2", "q0", "q1", "f1", "f2", "f3", "f4", "f5", "fd", "dsb", "st", "cexp"] \
-             + [n % i for i in range(RMAX) for n in ("dg%d", "aT%d", "aD%d")]
+              "sent", "arr2", "arrT2", "f1", "f2", "f3", "f4", "f5", "fd", "dsb", "st", "cexp"] \
+             + [n % i for i in range(RMAX) for n in ("dg%d", "aT%d", "aD%d", "q%d")]
 
 ALU, ACT, AX = AluOpType, ActivationFunctionType, AxisListType
 
@@ -65,16 +65,16 @@ def _plan(cores, topo):
         else:
             planes.append([c])
     mate = {a: b for a in cores for b in cores if topo.mates(a, b)}
-    lone = [c for c in cores if c not in mate]
+    groups = [q for p in planes for q in ([a for a in p if a in mate], [a for a in p if a not in mate]) if q]
     combs = []
-    for pi, p in enumerate(planes):
-        seats = [a for a in p if a in mate]
-        for i, a in enumerate(seats):
+    for gi, q in enumerate(groups):
+        for i, a in enumerate(q):
+            ds = [a] + [mate[a] if mate.get(a) in o else o[i] for o in groups if o is not q]
             x = [x for x in range(NSIM)
                  if topo.host(x) == topo.host(a) and topo.chip(x) == topo.chip(a) and topo.die(x) == topo.die(a)
-                 and x not in cores and topo.may_write(x, mate[a])][0]
-            combs.append((x, pi, [a, mate[a]] + [l for j, l in enumerate(lone) if j % len(seats) == i]))
-    return planes, combs
+                 and x not in cores and all(topo.may_write(x, d) for d in ds)][0]
+            combs.append((x, gi, ds))
+    return groups, combs
 
 
 def _hop2(x, dests, topo):
@@ -97,15 +97,15 @@ def _identity(g, T):
 
 
 def _rank_mask(c, topo, T):
-    planes, combs = _plan(T.cores, topo)
+    groups, combs = _plan(T.cores, topo)
     m = None
-    for x, pi, ds in combs:
-        if c in planes[pi]:
+    for x, gi, ds in combs:
+        if c in groups[gi]:
             m = topo.mask(c, x) if m is None else m & topo.mask(c, x)
     return m
 
 
-def _combiner(g, core, T, topo, srcs, pi, dests):
+def _combiner(g, core, T, topo, srcs, gi, dests):
     S, R = T.sem, len(srcs)
     v, s, t = g.vector, g.scalar, g.tensor
     need = [_count(_rank_mask(c, topo, T)) for c in srcs]
@@ -129,7 +129,7 @@ def _combiner(g, core, T, topo, srcs, pi, dests):
     v.tensor_copy(T.payT[:, 0:128], T.T_ps[:, 0:128]).then_inc(S.payT, 1)
     g.wait_ge(S.mu, 1)
     g.wait_ge(S.payT, 1)
-    send(T.payT[:], T.finT[:, pi * PW:(pi + 1) * PW], S.arrT2)
+    send(T.payT[:], T.finT[:, gi * PW:(gi + 1) * PW], S.arrT2)
     s.wait_ge(S.mu, 1)
     s.activation(T.cw[:, 0:R], mus, ACT.Exp, bias=T.payT[:, 128:129], scale=-1.0).then_inc(S.cexp, 1)
     v.wait_ge(S.id, 1)
@@ -149,22 +149,22 @@ def _combiner(g, core, T, topo, srcs, pi, dests):
     v.wait_ge(S.D, R)
     v.tensor_copy(T.pay[:], T.D_ps[:, 0:PW]).then_inc(S.payD, 1)
     g.wait_ge(S.payD, 1)
-    send(T.pay[:], T.fin[:, pi * PW:(pi + 1) * PW], S.arr2)
+    send(T.pay[:], T.fin[:, gi * PW:(gi + 1) * PW], S.arr2)
     g.wait_ge(S.sent, 2 * sum(_count(m) for m, ds in _hop2(core, dests, topo)))
 
 
 def rank_program(g, core, T, topo):
-    planes, combs = _plan(T.cores, topo)
-    for x, pi, ds in combs:
+    groups, combs = _plan(T.cores, topo)
+    for x, gi, ds in combs:
         if x == core:
-            _combiner(g, core, T, topo, planes[pi], pi, ds)
+            _combiner(g, core, T, topo, groups[gi], gi, ds)
             return
     if T.rank_of(core) is None:
         return
-    S = T.sem
+    S, NG = T.sem, len(groups)
     v, s, t = g.vector, g.scalar, g.tensor
-    mine = [pi for pi, p in enumerate(planes) if core in p][0]
-    slot = planes[mine].index(core)
+    mine = [gi for gi, q in enumerate(groups) if core in q][0]
+    slot = groups[mine].index(core)
 
     g.sync.dma_start(T.w_sb[:], T.w[:]).then_inc(S.ldw, 16)
     s.dma_start(T.h_sb[:], T.h[:]).then_inc(S.ldh, 16)
@@ -198,7 +198,7 @@ def rank_program(g, core, T, topo):
     v.wait_ge(S.D, 1)
     v.tensor_copy(T.pay[:], T.D_ps[:, 0:PW]).then_inc(S.payD, 1)
 
-    to = [x for x, pi, ds in combs if pi == mine]
+    to = [x for x, gi, ds in combs if gi == mine]
     m = _rank_mask(core, topo, T)
 
     def send(src, dst, sem):
@@ -212,40 +212,44 @@ def rank_program(g, core, T, topo):
     send(T.pay[:], T.land[:, slot * PW:(slot + 1) * PW], S["aD%d" % slot])
 
     need = 0
-    for x, pi, ds in combs:
+    for x, gi, ds in combs:
         for mk, dd in _hop2(x, ds, topo):
             if core in dd:
                 need += _count(mk)
-    mus = T.finT[:, 128:128 + PW + 1:PW]
-    ss = T.fin[:, 128:128 + PW + 1:PW]
+    mus = T.finT[:, 128:128 + PW * (NG - 1) + 1:PW]
+    ss = T.fin[:, 128:128 + PW * (NG - 1) + 1:PW]
     t.wait_ge(S.arrT2, need)
-    t.matmul(T.f_ps[:, 0:128], T.finT[:, 0:128], T.ident[:], True, False)
-    t.matmul(T.f_ps[:, 0:128], T.finT[:, PW:PW + 128], T.ident[:], False, False)
+    for p in range(NG):
+        t.matmul(T.f_ps[:, 0:128], T.finT[:, p * PW:p * PW + 128], T.ident[:], p == 0, False)
     v.wait_ge(S.arrT2, need)
     v.tensor_reduce(T.nm[:], mus, AX.X, ALU.min).then_inc(S.f1, 1)
     s.wait_ge(S.arrT2, need)
     s.wait_ge(S.f1, 1)
-    s.activation(T.cw[:, 0:2], mus, ACT.Exp, bias=T.nm[:], scale=-1.0).then_inc(S.f2, 1)
+    s.activation(T.cw[:, 0:NG], mus, ACT.Exp, bias=T.nm[:], scale=-1.0).then_inc(S.f2, 1)
     v.wait_ge(S.f2, 1)
     v.wait_ge(S.id, 1)
-    for p in range(2):
+    for p in range(NG):
         v.tensor_scalar(T.diag[:, p * 128:(p + 1) * 128], T.ident[:], T.cw[:, p:p + 1], None, ALU.mult).then_inc(S["dg%d" % p], 1)
     v.wait_ge(S.arr2, need)
-    v.tensor_tensor(T.cs[:], T.cw[:, 0:2], ss, ALU.mult).then_inc(S.f3, 1)
+    v.tensor_tensor(T.cs[:, 0:NG], T.cw[:, 0:NG], ss, ALU.mult).then_inc(S.f3, 1)
     v.wait_ge(S.f3, 1)
-    v.tensor_reduce(T.ssum[:], T.cs[:], AX.X, ALU.add).then_inc(S.f4, 1)
+    v.tensor_reduce(T.ssum[:], T.cs[:, 0:NG], AX.X, ALU.add).then_inc(S.f4, 1)
     v.wait_ge(S.f4, 1)
     v.reciprocal(T.rs[:], T.ssum[:]).then_inc(S.f5, 1)
     v.wait_ge(S.f5, 1)
-    v.wait_ge(S.dg0, 1)
-    v.tensor_scalar(T.dq[:, 0:128], T.diag[:, 0:128], T.rs[:], None, ALU.mult).then_inc(S.q0, 1)
     s.wait_ge(S.f5, 1)
-    s.wait_ge(S.dg1, 1)
-    s.activation(T.dq[:, 128:256], T.diag[:, 128:256], ACT.Copy, scale=T.rs[:]).then_inc(S.q1, 1)
+    for p in range(NG):
+        o, i = T.dq[:, p * 128:(p + 1) * 128], T.diag[:, p * 128:(p + 1) * 128]
+        if p % 2 == 0:
+            v.wait_ge(S["dg%d" % p], 1)
+            v.tensor_scalar(o, i, T.rs[:], None, ALU.mult).then_inc(S["q%d" % p], 1)
+        else:
+            s.wait_ge(S["dg%d" % p], 1)
+            s.activation(o, i, ACT.Copy, scale=T.rs[:]).then_inc(S["q%d" % p], 1)
     t.wait_ge(S.arr2, need)
-    for p in range(2):
+    for p in range(NG):
         t.wait_ge(S["q%d" % p], 1)
-        i = t.matmul(T.f_ps[:, 0:128], T.fin[:, p * PW:p * PW + 128], T.dq[:, p * 128:(p + 1) * 128], False, p == 1)
+        i = t.matmul(T.f_ps[:, 0:128], T.fin[:, p * PW:p * PW + 128], T.dq[:, p * 128:(p + 1) * 128], False, p == NG - 1)
     i.then_inc(S.fd, 1)
     v.wait_ge(S.fd, 1)
     v.tensor_copy(T.d_sb[:], T.f_ps[:, 0:128]).then_inc(S.dsb, 1)

from concourse.bass import DstId, RemoteDMATransfer
from concourse.mybir import AluOpType, AxisListType, ActivationFunctionType

NSIM = 256
PW = 129
RMAX = 4

SCRATCH = {
    "h_sb": ("sbuf", [128, 128], "bfloat16"),
    "w_sb": ("sbuf", [128, 128], "bfloat16"),
    "oh_sb": ("sbuf", [128, 128], "bfloat16"),
    "ones": ("sbuf", [128, 128], "bfloat16"),
    "ident": ("sbuf", [128, 128], "bfloat16"),
    "wT1": ("sbuf", [128, 136], "bfloat16"),
    "eT_sb": ("sbuf", [128, 128], "bfloat16"),
    "e_sb": ("sbuf", [128, 128], "bfloat16"),
    "pay": ("sbuf", [128, PW], "bfloat16"),
    "payT": ("sbuf", [128, PW], "bfloat16"),
    "land": ("sbuf", [128, RMAX * PW], "bfloat16"),
    "landT": ("sbuf", [128, RMAX * PW], "bfloat16"),
    "fin": ("sbuf", [128, RMAX * PW], "bfloat16"),
    "finT": ("sbuf", [128, RMAX * PW], "bfloat16"),
    "cw": ("sbuf", [128, RMAX], "float32"),
    "diag": ("sbuf", [128, RMAX * 128], "bfloat16"),
    "dq": ("sbuf", [128, RMAX * 128], "bfloat16"),
    "nm": ("sbuf", [128, 1], "float32"),
    "cs": ("sbuf", [128, RMAX], "float32"),
    "ssum": ("sbuf", [128, 1], "float32"),
    "rs": ("sbuf", [128, 1], "float32"),
    "d_sb": ("sbuf", [128, 128], "bfloat16"),
    "z_ps": ("psum", [128, 512], "float32"),
    "wT_ps": ("psum", [128, 1024], "bfloat16"),
    "e_ps": ("psum", [128, 1024], "bfloat16"),
    "D_ps": ("psum", [128, 512], "float32"),
    "T_ps": ("psum", [128, 512], "float32"),
    "f_ps": ("psum", [128, 512], "float32"),
}
SEMAPHORES = ["ones", "id", "onec", "ldw", "ldh", "ldoh", "z", "wTp", "wTs", "mu", "eT", "ep", "e", "D", "payD", "Tp", "payT",
              "sent", "arr2", "arrT2", "f1", "f2", "f3", "f4", "f5", "fd", "dsb", "st", "cexp"] \
             + [n % i for i in range(RMAX) for n in ("dg%d", "aT%d", "aD%d", "q%d")]

ALU, ACT, AX = AluOpType, ActivationFunctionType, AxisListType


def _take(mask, n):
    out, left = 0, n
    for i in range(mask.bit_length()):
        if left and (mask >> i) & 1:
            out |= 1 << i
            left -= 1
    return out


def _count(mask):
    return sum((mask >> i) & 1 for i in range(mask.bit_length()))


def _plan(cores, topo):
    planes = []
    for c in cores:
        for p in planes:
            if topo.same_plane(p[0], c):
                p.append(c)
                break
        else:
            planes.append([c])
    mate = {a: b for a in cores for b in cores if topo.mates(a, b)}
    groups = [q for p in planes for q in ([a for a in p if a in mate], [a for a in p if a not in mate]) if q]
    combs = []
    for gi, q in enumerate(groups):
        for i, a in enumerate(q):
            ds = [a] + [mate[a] if mate.get(a) in o else o[i] for o in groups if o is not q]
            x = [x for x in range(NSIM)
                 if topo.host(x) == topo.host(a) and topo.chip(x) == topo.chip(a) and topo.die(x) == topo.die(a)
                 and x not in cores and all(topo.may_write(x, d) for d in ds)][0]
            combs.append((x, gi, ds))
    return groups, combs


def _hop2(x, dests, topo):
    full = topo.mask(x, dests[0])
    low = full
    for d in dests[1:]:
        low &= topo.mask(x, d)
    return [(_take(full & ~low, 4), dests[:1]), (low, dests[1:])]


def _dst(d, src, topo):
    rid, pid = topo.addr(d, src)
    return DstId(rid=rid, pnc=pid)


def _identity(g, T):
    g.vector.memset(T.ones[:], 1.0).then_inc(T.sem.ones, 1)
    g.wait_ge(T.sem.ones, 1)
    g.affine_select(T.ident[:], T.ones[:], [[-1, 128]], ALU.is_equal, 0.0, 0, 1).then_inc(T.sem.id, 1)


def _rank_mask(c, topo, T):
    groups, combs = _plan(T.cores, topo)
    m = None
    for x, gi, ds in combs:
        if c in groups[gi]:
            m = topo.mask(c, x) if m is None else m & topo.mask(c, x)
    return m


def _combiner(g, core, T, topo, srcs, gi, dests):
    S, R = T.sem, len(srcs)
    v, s, t = g.vector, g.scalar, g.tensor
    need = [_count(_rank_mask(c, topo, T)) for c in srcs]
    _identity(g, T)
    mus = T.landT[:, 128:128 + PW * (R - 1) + 1:PW]

    def send(src, dst, sem):
        g.remote_dma_fused([RemoteDMATransfer(dst_ids=[_dst(d, core, topo) for d in ds], dma_engine_mask=m, remote_sem=sem,
                                              srcs=[src], dsts=[dst for d in ds], alu_op=0)
                            for m, ds in _hop2(core, dests, topo)], local_sem=S.sent)

    t.wait_ge(S.id, 1)
    for r in range(R):
        t.wait_ge(S["aT%d" % r], need[r])
        t.matmul(T.T_ps[:, 0:128], T.ident[:], T.landT[:, r * PW:r * PW + 128], r == 0, r == R - 1).then_inc(S.Tp, 1)
    for r in range(R):
        v.wait_ge(S["aT%d" % r], need[r])
        s.wait_ge(S["aT%d" % r], need[r])
    v.tensor_reduce(T.payT[:, 128:129], mus, AX.X, ALU.min).then_inc(S.mu, 1)
    v.wait_ge(S.Tp, R)
    v.tensor_copy(T.payT[:, 0:128], T.T_ps[:, 0:128]).then_inc(S.payT, 1)
    g.wait_ge(S.mu, 1)
    g.wait_ge(S.payT, 1)
    send(T.payT[:], T.finT[:, gi * PW:(gi + 1) * PW], S.arrT2)
    s.wait_ge(S.mu, 1)
    s.activation(T.cw[:, 0:R], mus, ACT.Exp, bias=T.payT[:, 128:129], scale=-1.0).then_inc(S.cexp, 1)
    v.wait_ge(S.id, 1)
    v.wait_ge(S.cexp, 1)
    s.wait_ge(S.id, 1)
    s.wait_ge(S.cexp, 1)
    for r in range(R):
        o = T.diag[:, r * 128:(r + 1) * 128]
        if r % 2 == 0:
            v.tensor_scalar(o, T.ident[:], T.cw[:, r:r + 1], None, ALU.mult).then_inc(S["dg%d" % r], 1)
        else:
            s.activation(o, T.ident[:], ACT.Copy, scale=T.cw[:, r:r + 1]).then_inc(S["dg%d" % r], 1)
    for r in range(R):
        t.wait_ge(S["dg%d" % r], 1)
        t.wait_ge(S["aD%d" % r], need[r])
        t.matmul(T.D_ps[:, 0:PW], T.diag[:, r * 128:(r + 1) * 128], T.land[:, r * PW:(r + 1) * PW], r == 0, r == R - 1).then_inc(S.D, 1)
    v.wait_ge(S.D, R)
    v.tensor_copy(T.pay[:], T.D_ps[:, 0:PW]).then_inc(S.payD, 1)
    g.wait_ge(S.payD, 1)
    send(T.pay[:], T.fin[:, gi * PW:(gi + 1) * PW], S.arr2)
    g.wait_ge(S.sent, 2 * sum(_count(m) for m, ds in _hop2(core, dests, topo)))


def rank_program(g, core, T, topo):
    groups, combs = _plan(T.cores, topo)
    for x, gi, ds in combs:
        if x == core:
            _combiner(g, core, T, topo, groups[gi], gi, ds)
            return
    if T.rank_of(core) is None:
        return
    S, NG = T.sem, len(groups)
    v, s, t = g.vector, g.scalar, g.tensor
    mine = [gi for gi, q in enumerate(groups) if core in q][0]
    slot = groups[mine].index(core)

    g.sync.dma_start(T.w_sb[:], T.w[:]).then_inc(S.ldw, 16)
    s.dma_start(T.h_sb[:], T.h[:]).then_inc(S.ldh, 16)
    g.sync.dma_start(T.oh_sb[:], T.oh[:]).then_inc(S.ldoh, 16)
    _identity(g, T)
    v.memset(T.wT1[:, 128:129], 1.0).then_inc(S.onec, 1)

    t.wait_ge(S.ldw, 16)
    t.wait_ge(S.ldh, 16)
    t.matmul(T.z_ps[:, 0:128], T.h_sb[:], T.w_sb[:], True, True).then_inc(S.z, 1)
    t.wait_ge(S.id, 1)
    t.transpose(T.wT_ps[:, 0:128], T.w_sb[:], T.ident[:]).then_inc(S.wTp, 1)
    v.wait_ge(S.z, 1)
    v.tensor_reduce(T.payT[:, 128:129], T.z_ps[:, 0:128], AX.X, ALU.max, negate=True).then_inc(S.mu, 1)
    s.wait_ge(S.mu, 1)
    s.activation(T.eT_sb[:], T.z_ps[:, 0:128], ACT.Exp, bias=T.payT[:, 128:129]).then_inc(S.eT, 1)
    v.wait_ge(S.wTp, 1)
    v.tensor_copy(T.wT1[:, 0:128], T.wT_ps[:, 0:128]).then_inc(S.wTs, 1)
    t.wait_ge(S.wTs, 1)
    t.wait_ge(S.ldoh, 16)
    t.matmul(T.T_ps[:, 0:128], T.oh_sb[:], T.wT1[:, 0:128], True, True).then_inc(S.Tp, 1)
    v.wait_ge(S.Tp, 1)
    v.tensor_scalar(T.payT[:, 0:128], T.T_ps[:, 0:128], -1.0, None, ALU.mult).then_inc(S.payT, 1)
    t.wait_ge(S.eT, 1)
    t.transpose(T.e_ps[:, 0:128], T.eT_sb[:], T.ident[:]).then_inc(S.ep, 1)
    v.wait_ge(S.ep, 1)
    v.tensor_copy(T.e_sb[:], T.e_ps[:, 0:128]).then_inc(S.e, 1)
    t.wait_ge(S.e, 1)
    t.wait_ge(S.onec, 1)
    t.matmul(T.D_ps[:, 0:PW], T.e_sb[:], T.wT1[:, 0:PW], True, True).then_inc(S.D, 1)
    v.wait_ge(S.D, 1)
    v.tensor_copy(T.pay[:], T.D_ps[:, 0:PW]).then_inc(S.payD, 1)

    to = [x for x, gi, ds in combs if gi == mine]
    m = _rank_mask(core, topo, T)

    def send(src, dst, sem):
        g.remote_dma_fused([RemoteDMATransfer(dst_ids=[_dst(x, core, topo) for x in to], dma_engine_mask=m, remote_sem=sem,
                                              srcs=[src], dsts=[dst for x in to], alu_op=0)], local_sem=S.sent)

    g.wait_ge(S.mu, 1)
    g.wait_ge(S.payT, 1)
    send(T.payT[:], T.landT[:, slot * PW:(slot + 1) * PW], S["aT%d" % slot])
    g.wait_ge(S.payD, 1)
    send(T.pay[:], T.land[:, slot * PW:(slot + 1) * PW], S["aD%d" % slot])

    need = 0
    for x, gi, ds in combs:
        for mk, dd in _hop2(x, ds, topo):
            if core in dd:
                need += _count(mk)
    mus = T.finT[:, 128:128 + PW * (NG - 1) + 1:PW]
    ss = T.fin[:, 128:128 + PW * (NG - 1) + 1:PW]
    t.wait_ge(S.arrT2, need)
    for p in range(NG):
        t.matmul(T.f_ps[:, 0:128], T.finT[:, p * PW:p * PW + 128], T.ident[:], p == 0, False)
    v.wait_ge(S.arrT2, need)
    v.tensor_reduce(T.nm[:], mus, AX.X, ALU.min).then_inc(S.f1, 1)
    s.wait_ge(S.arrT2, need)
    s.wait_ge(S.f1, 1)
    s.activation(T.cw[:, 0:NG], mus, ACT.Exp, bias=T.nm[:], scale=-1.0).then_inc(S.f2, 1)
    v.wait_ge(S.f2, 1)
    v.wait_ge(S.id, 1)
    for p in range(NG):
        v.tensor_scalar(T.diag[:, p * 128:(p + 1) * 128], T.ident[:], T.cw[:, p:p + 1], None, ALU.mult).then_inc(S["dg%d" % p], 1)
    v.wait_ge(S.arr2, need)
    v.tensor_tensor(T.cs[:, 0:NG], T.cw[:, 0:NG], ss, ALU.mult).then_inc(S.f3, 1)
    v.wait_ge(S.f3, 1)
    v.tensor_reduce(T.ssum[:], T.cs[:, 0:NG], AX.X, ALU.add).then_inc(S.f4, 1)
    v.wait_ge(S.f4, 1)
    v.reciprocal(T.rs[:], T.ssum[:]).then_inc(S.f5, 1)
    v.wait_ge(S.f5, 1)
    s.wait_ge(S.f5, 1)
    for p in range(NG):
        o, i = T.dq[:, p * 128:(p + 1) * 128], T.diag[:, p * 128:(p + 1) * 128]
        if p % 2 == 0:
            v.wait_ge(S["dg%d" % p], 1)
            v.tensor_scalar(o, i, T.rs[:], None, ALU.mult).then_inc(S["q%d" % p], 1)
        else:
            s.wait_ge(S["dg%d" % p], 1)
            s.activation(o, i, ACT.Copy, scale=T.rs[:]).then_inc(S["q%d" % p], 1)
    t.wait_ge(S.arr2, need)
    for p in range(NG):
        t.wait_ge(S["q%d" % p], 1)
        i = t.matmul(T.f_ps[:, 0:128], T.fin[:, p * PW:p * PW + 128], T.dq[:, p * 128:(p + 1) * 128], False, p == NG - 1)
    i.then_inc(S.fd, 1)
    v.wait_ge(S.fd, 1)
    v.tensor_copy(T.d_sb[:], T.f_ps[:, 0:128]).then_inc(S.dsb, 1)
    g.sync.wait_ge(S.dsb, 1)
    g.sync.dma_start(T.d[:], T.d_sb[:]).then_inc(S.st, 16)
    g.sync.wait_ge(S.st, 16)
    g.wait_ge(S.sent, 2 * _count(m))
